import numpy as np
import ml_dtypes


def mxq(x, axis, fmt="e4m3"):
    dtype, down = {"e4m3": (ml_dtypes.float8_e4m3fn, 7), "e5m2": (ml_dtypes.float8_e5m2, 14)}[fmt]
    v = np.moveaxis(np.asarray(x, np.float32).astype(ml_dtypes.bfloat16).astype(np.float64), axis, -1)
    blocks = v.reshape(v.shape[:-1] + (-1, 32))
    amax = np.abs(blocks).max(-1, keepdims=True)
    byte = np.maximum(np.where(amax > 0, np.frexp(amax)[1] - 1 + 127, 0) - down, 1)
    scale = np.exp2(byte - 127.0)
    codes = (blocks / scale).astype(np.float32).astype(dtype).astype(np.float64)
    return np.moveaxis((codes * scale).reshape(v.shape), -1, axis)


WIDE = False


def mx_kscale(k):
    if not WIDE:
        return np.ones(k)
    levels = np.array([10, -10, 5, -5, 0])
    if k % 512:
        return np.exp2(np.random.permutation(np.resize(levels, k // 32))).repeat(32)
    a = np.empty((k // 512, 16))
    for p in range(k // 512):
        a[p, :8] = np.random.permutation(np.resize(levels, 8))
        for g in range(8):
            far = levels[np.abs(levels - a[p, g]) >= 10]
            a[p, g + 8] = far[np.random.randint(len(far))]
    return np.exp2(a.ravel()).repeat(32)


def f64(x):
    return np.asarray(x).astype(np.float64)


def striped(idx):
    return np.tile(np.asarray(idx).reshape(-1, 16).T, (8, 1)).astype(np.uint16)


def unstriped(offs):
    return offs[:16].T.reshape(-1).astype(np.int64)


E2M1 = np.array([0.0, 0.5, 1.0, 1.5, 2.0, 3.0, 4.0, 6.0, -0.0, -0.5, -1.0, -1.5, -2.0, -3.0, -4.0, -6.0])


def pack_weight(w, fmt):
    k, n = w.shape
    w = f64(np.asarray(w, np.float32).astype(ml_dtypes.bfloat16)).reshape(k // 32, 32, n)
    amax = np.abs(w).max(1)
    if fmt == "e4m3":
        byte = np.frexp(amax)[1] - 1 + 127 - 7
    else:
        mant, ex = np.frexp(amax / 6.0)
        byte = np.where(mant > 0.5, ex, ex - 1) + 127
    byte = np.clip(np.where(amax > 0, byte, 1), 1, 254)
    scaled = (w * np.exp2(127.0 - byte)[:, None, :]).reshape(k, n).astype(np.float32)
    by_word = np.ascontiguousarray(scaled.reshape(k // 512, 128, 4, n).transpose(0, 1, 3, 2))
    if fmt == "e4m3":
        words = by_word.astype(ml_dtypes.float8_e4m3fn).view(np.uint8)
    else:
        c = by_word.astype(ml_dtypes.float4_e2m1fn).view(np.uint8) & 0xF
        words = (c[..., 0::2] | (c[..., 1::2] << 4)).reshape(k // 512, 128, 2 * n)
    return np.ascontiguousarray(words), np.ascontiguousarray(byte.astype(np.uint8).reshape(k // 512, 16, n))


def unpack_weight(words, scales, fmt):
    g, _, n = scales.shape
    words = np.ascontiguousarray(words).reshape(g, 128, n, -1)
    if fmt == "e4m3":
        vals = words.view(ml_dtypes.float8_e4m3fn).astype(np.float64)
    else:
        nib = np.empty((g, 128, n, 4), np.uint8)
        nib[..., 0::2] = words & 0xF
        nib[..., 1::2] = words >> 4
        vals = E2M1[nib]
    vals = vals * np.repeat(np.exp2(scales.astype(np.float64) - 127.0), 8, axis=1)[..., None]
    return vals.transpose(0, 1, 3, 2).reshape(g * 512, n)


K, T, J, R, V, C, N = 512, 1024, 256, 512, 1024, 512, 256


def setup_inputs():
    n = np.random.standard_normal
    idx = np.random.permutation(T)[:J]
    idx2 = np.random.permutation(V)[:R]
    idx3 = np.random.permutation(C)[:J]
    idx4 = np.random.permutation(C)[:J]
    fk = mx_kscale(K)
    fr = mx_kscale(R)
    tr = np.ones(V)
    tr[idx2] = fr
    wtp = pack_weight(n((K, V)) * 1 / np.sqrt(K) / fk[:, None] * tr, "e2m1")
    wbp = pack_weight(n((R, N)) * 1 / np.sqrt(R) / fr[:, None], "e2m1")
    return {
        "cq": (np.random.randint(-7, 8, (K, T)).astype(np.float64)).astype(np.float32),
        "ga": (np.random.uniform(0.1, 0.4, (K, 1)) * fk[:, None]).astype(np.float32),
        "wt_words": wtp[0],
        "wt_scales": wtp[1],
        "sa": (np.random.uniform(0.5, 1.6, (R, 1))).astype(np.float32),
        "wb_words": wbp[0],
        "wb_scales": wbp[1],
        "offs": striped(idx),
        "offs2": striped(idx2),
        "offs3": striped(idx3),
        "offs4": striped(idx4),
    }


def reference(cq, ga, wt_words, wt_scales, sa, wb_words, wb_scales, offs, offs2, offs3, offs4):
    idx = unstriped(offs)
    idx2 = unstriped(offs2)
    idx3 = unstriped(offs3)
    idx4 = unstriped(offs4)
    wtu = unpack_weight(wt_words, wt_scales, "e2m1")
    wbu = unpack_weight(wb_words, wb_scales, "e2m1")
    x1 = f64(cq)[:, idx] * f64(ga)
    wtidx2g = wtu[:, idx2]
    x1q = mxq(x1, 0, "e4m3")
    a = wtidx2g.T @ x1q
    pw = np.zeros((R, C))
    pw[:, idx3] = a
    hid = np.maximum(pw[:, idx4] * f64(sa), a)
    hidq = mxq(hid, 0, "e4m3")
    y = wbu.T @ hidq
    return y

@@ -1,0 +1,179 @@
+from contextlib import ExitStack
+
+import concourse.mybir as mybir
+
+K, T, J, R, V, C, N = 512, 1024, 256, 512, 1024, 512, 256
+FLOPS = 2 * K * R * J + 2 * R * N * J
+
+F32 = mybir.dt.float32
+BF16 = mybir.dt.bfloat16
+I32 = mybir.dt.int32
+U32 = mybir.dt.uint32
+U16 = mybir.dt.uint16
+U8 = mybir.dt.uint8
+FP8X4 = mybir.dt.float8_e4m3fn_x4
+FP4X4 = mybir.dt.float4_e2m1fn_x4
+COPY = mybir.ActivationFunctionType.Copy
+MAX = mybir.AluOpType.max
+
+P = 128
+PACK = 4
+QUADS = 4
+HALF = J // 2
+SPLIT = 64
+
+
+def spread_scale_rows(nc, plane, stage):
+    width = plane.shape[1] // 4
+    for q in range(QUADS):
+        nc.vector.tensor_copy(
+            out=plane[:].bitcast(I32)[32 * q : 32 * q + 4, :],
+            in_=stage[:, q * width : (q + 1) * width],
+        )
+
+
+def tile_list_boardownweighed_codedstore_one_plain_kernel(
+    tc, cq, ga, wt_words, wt_scales, sa, wb_words, wb_scales, offs, offs2, offs3, offs4, out
+):
+    nc = tc.nc
+    with ExitStack() as ctx:
+        keep = ctx.enter_context(tc.tile_pool(name="keep", bufs=1))
+        psum = ctx.enter_context(tc.psum_pool(name="psum", bufs=1))
+
+        list_x = keep.tile([P, J // 16], U16)
+        list_w = keep.tile([P, R // 16], U16)
+        list_put = keep.tile([P, J // 16], U16)
+        list_get = keep.tile([P, J // 16], U16)
+        wt_win = keep.tile([P, V], U16, align_bytes=64)
+        wt_stage = keep.tile([4, QUADS * V // 4], I32, align_bytes=64)
+        wb_codes = keep.tile([P, 2 * N], U8, align_bytes=64)
+        steps = keep.tile([P, PACK], F32)
+        weights = keep.tile([P, PACK], F32)
+        cq_rows = [keep.tile([P, T], F32, name="cq%d" % t, align_bytes=64) for t in range(PACK)]
+        cq_planes = cq.rearrange("(p t) c -> t p c", t=PACK)
+
+        nc.sync.dma_start(out=wt_win[:].bitcast(I32), in_=wt_words[0].bitcast(I32))
+        nc.sync.dma_start(out=cq_rows[0][:], in_=cq_planes[0])
+        nc.sync.dma_start(list_w[:], offs2)
+        nc.sync.dma_start(
+            out=wt_stage[:].rearrange("r (q c) -> r q c", q=QUADS),
+            in_=wt_scales[0].bitcast(I32).rearrange("(q r) c -> r q c", q=QUADS),
+        )
+        nc.sync.dma_start(list_x[:], offs)
+        nc.sync.dma_start(out=steps[:], in_=ga.rearrange("(p t) o -> p (t o)", t=PACK))
+        for t in range(1, PACK):
+            nc.sync.dma_start(out=cq_rows[t][:], in_=cq_planes[t])
+        nc.sync.dma_start(out=weights[:], in_=sa.rearrange("(p t) o -> p (t o)", t=PACK))
+        nc.sync.dma_start(list_put[:], offs3)
+        nc.sync.dma_start(list_get[:], offs4)
+        nc.sync.dma_start(out=wb_codes[:].bitcast(I32), in_=wb_words[0].bitcast(I32))
+
+        wt_plane = keep.tile([P, V], U8, align_bytes=64)
+        wb_plane = keep.tile([P, N], U8, align_bytes=64)
+        nc.vector.memset(wt_plane[:].bitcast(I32), 0)
+        nc.vector.memset(wb_plane[:].bitcast(I32), 0)
+        for q in range(QUADS):
+            nc.sync.dma_start(
+                out=wb_plane[:].bitcast(I32)[32 * q : 32 * q + 4, :],
+                in_=wb_scales[0].bitcast(I32)[4 * q : 4 * q + 4, :],
+            )
+        boards = [keep.tile([P, C], F32, name="board%d" % t, align_bytes=64) for t in range(PACK)]
+        for t in range(PACK):
+            nc.vector.memset(boards[t][:], 0.0)
+
+        wt_picked = keep.tile([P, R], U16, align_bytes=64)
+        wt_codes = keep.tile([P, PACK, P], U16, align_bytes=64)
+        wt_bytes = keep.tile([P, PACK, P], U8, align_bytes=64)
+        nc.vector.tensor_copy(wt_picked[:], wt_win[:].indirect(list_w[:]))
+        nc.vector.tensor_copy(out=wt_codes[:], in_=wt_picked[:].rearrange("p (q t) -> p t q", t=PACK))
+        spread_scale_rows(nc, wt_plane, wt_stage)
+        nc.vector.tensor_copy(wt_bytes[:].rearrange("p t q -> p q t"), wt_plane[:].indirect(list_w[:]))
+
+        x_planes = keep.tile([P, PACK, J], BF16, align_bytes=64)
+        for t in range(PACK):
+            nc.scalar.activation(
+                out=x_planes[:, t, :], in_=cq_rows[t][:].indirect(list_x[:]), func=COPY, scale=steps[:, t : t + 1]
+            )
+        x_woven = keep.tile([P, J, PACK], BF16, align_bytes=64)
+        nc.vector.tensor_copy(
+            out=x_woven[:].rearrange("p (c i) t -> p c t i", i=4),
+            in_=x_planes[:].rearrange("p t (c i) -> p c t i", i=4),
+        )
+        x_codes = keep.tile([P, J], U32, align_bytes=64)
+        x_scales = keep.tile([P, J], U8, align_bytes=64)
+        nc.vector.quantize_mx(
+            out=x_codes[:].bitcast(FP8X4), scales=x_scales[:], in_=x_woven[:].rearrange("p j t -> p (j t)")
+        )
+
+        own = keep.tile([P, PACK, J], F32, align_bytes=64)
+        read = keep.tile([P, PACK, J], F32, align_bytes=64)
+        sums = [psum.tile([P, J], F32, name="a%d" % t) for t in range(PACK)]
+        for t in range(PACK):
+            nc.tensor.matmul_mx(
+                out=sums[t][:],
+                lhsT=wt_codes[:, t, :].bitcast(U8).bitcast(FP4X4),
+                lhsT_scale=wt_bytes[:, t, :],
+                rhs=x_codes[:].bitcast(FP8X4),
+                rhs_scale=x_scales[:],
+                start=True,
+                stop=True,
+            )
+
+        def fetch(t, lo, hi):
+            nc.scalar.activation(
+                out=read[:, t, lo:hi],
+                in_=boards[t][:].indirect(list_get[:, lo // 16 : hi // 16]),
+                func=COPY,
+                scale=weights[:, t : t + 1],
+            )
+
+        nc.vector.tensor_copy(out=own[:, 0, :], in_=sums[0][:])
+        nc.scalar.copy(out=own[:, 1, :], in_=sums[1][:])
+        nc.vector.tensor_copy(boards[0][:].indirect(list_put[:]), own[:, 0, :])
+        nc.scalar.activation(out=boards[1][:].indirect(list_put[:]), in_=own[:, 1, :], func=COPY)
+        nc.vector.tensor_copy(out=own[:, 2, :], in_=sums[2][:])
+        nc.scalar.copy(out=own[:, 3, :], in_=sums[3][:])
+        nc.vector.tensor_copy(boards[2][:].indirect(list_put[:]), own[:, 2, :])
+        nc.scalar.activation(
+            out=boards[3][:].indirect(list_put[:, 0 : SPLIT // 16]), in_=own[:, 3, 0:SPLIT], func=COPY
+        )
+        nc.vector.tensor_copy(boards[3][:].indirect(list_put[:, SPLIT // 16 : J // 16]), own[:, 3, SPLIT:J])
+        for t in range(PACK - 1):
+            fetch(t, 0, J)
+        for h in range(2):
+            fetch(PACK - 1, h * HALF, (h + 1) * HALF)
+
+        out_rows = out.rearrange("(m p) j -> p m j", p=P)
+        woven = [keep.tile([P, HALF, PACK], BF16, name="hid%d" % h, align_bytes=64) for h in range(2)]
+        for h in range(2):
+            cols = slice(h * HALF, (h + 1) * HALF)
+            nc.vector.tensor_tensor(
+                out=woven[h][:].rearrange("p (c i) t -> p c t i", i=4),
+                in0=read[:, :, cols].rearrange("p t (c i) -> p c t i", i=4),
+                in1=own[:, :, cols].rearrange("p t (c i) -> p c t i", i=4),
+                op=MAX,
+            )
+        for h in range(2):
+            cols = slice(h * HALF, (h + 1) * HALF)
+            h_codes = keep.tile([P, HALF], U32, name="h_codes%d" % h, align_bytes=64)
+            h_scales = keep.tile([P, HALF], U8, name="h_scales%d" % h, align_bytes=64)
+            nc.vector.quantize_mx(
+                out=h_codes[:].bitcast(FP8X4), scales=h_scales[:], in_=woven[h][:].rearrange("p j t -> p (j t)")
+            )
+            result = keep.tile([P, N // P, HALF], F32, name="result%d" % h, align_bytes=64)
+            for m in range(N // P):
+                y = psum.tile([P, HALF], F32, name="y%d%d" % (h, m))
+                nc.tensor.matmul_mx(
+                    out=y[:],
+                    lhsT=wb_codes[:, 2 * P * m : 2 * P * (m + 1)].bitcast(FP4X4),
+                    lhsT_scale=wb_plane[:, P * m : P * (m + 1)],
+                    rhs=h_codes[:].bitcast(FP8X4),
+                    rhs_scale=h_scales[:],
+                    start=True,
+                    stop=True,
+                )
+                if h == 1 and m == 1:
+                    nc.vector.tensor_copy(out=result[:, m, :], in_=y[:])
+                else:
+                    nc.scalar.copy(out=result[:, m, :], in_=y[:])
+            nc.sync.dma_start(out=out_rows[:, :, cols], in_=result[:])

@@ -20,7 +20,8 @@ P = 128
 PACK = 4
 QUADS = 4
 HALF = J // 2
-SPLIT = 64
+SPLIT = 192
+WEAVE_SPLIT = 192
 
 
 def spread_scale_rows(nc, plane, stage):
@@ -52,15 +53,15 @@ def tile_list_boardownweighed_codedstore_one_plain_kernel(
         cq_rows = [keep.tile([P, T], F32, name="cq%d" % t, align_bytes=64) for t in range(PACK)]
         cq_planes = cq.rearrange("(p t) c -> t p c", t=PACK)
 
-        nc.sync.dma_start(out=wt_win[:].bitcast(I32), in_=wt_words[0].bitcast(I32))
         nc.sync.dma_start(out=cq_rows[0][:], in_=cq_planes[0])
+        nc.sync.dma_start(list_x[:], offs)
+        nc.sync.dma_start(out=steps[:], in_=ga.rearrange("(p t) o -> p (t o)", t=PACK))
+        nc.sync.dma_start(out=wt_win[:].bitcast(I32), in_=wt_words[0].bitcast(I32))
         nc.sync.dma_start(list_w[:], offs2)
         nc.sync.dma_start(
             out=wt_stage[:].rearrange("r (q c) -> r q c", q=QUADS),
             in_=wt_scales[0].bitcast(I32).rearrange("(q r) c -> r q c", q=QUADS),
         )
-        nc.sync.dma_start(list_x[:], offs)
-        nc.sync.dma_start(out=steps[:], in_=ga.rearrange("(p t) o -> p (t o)", t=PACK))
         for t in range(1, PACK):
             nc.sync.dma_start(out=cq_rows[t][:], in_=cq_planes[t])
         nc.sync.dma_start(out=weights[:], in_=sa.rearrange("(p t) o -> p (t o)", t=PACK))
@@ -94,30 +95,57 @@ def tile_list_boardownweighed_codedstore_one_plain_kernel(
             nc.scalar.activation(
                 out=x_planes[:, t, :], in_=cq_rows[t][:].indirect(list_x[:]), func=COPY, scale=steps[:, t : t + 1]
             )
-        x_woven = keep.tile([P, J, PACK], BF16, align_bytes=64)
-        nc.vector.tensor_copy(
-            out=x_woven[:].rearrange("p (c i) t -> p c t i", i=4),
-            in_=x_planes[:].rearrange("p t (c i) -> p c t i", i=4),
-        )
+        x_woven = [keep.tile([P, HALF, PACK], BF16, name="x_woven%d" % h, align_bytes=64) for h in range(2)]
+
+        def weave(copy, lo, hi):
+            h, base = lo // HALF, lo // HALF * HALF
+            copy(
+                out=x_woven[h][:, lo - base : hi - base, :].rearrange("p (c i) t -> p c t i", i=4),
+                in_=x_planes[:, :, lo:hi].rearrange("p t (c i) -> p c t i", i=4),
+            )
+
+        weave(nc.vector.tensor_copy, 0, HALF)
+        weave(nc.vector.tensor_copy, HALF, WEAVE_SPLIT)
+        weave(nc.scalar.copy, WEAVE_SPLIT, J)
         x_codes = keep.tile([P, J], U32, align_bytes=64)
         x_scales = keep.tile([P, J], U8, align_bytes=64)
-        nc.vector.quantize_mx(
-            out=x_codes[:].bitcast(FP8X4), scales=x_scales[:], in_=x_woven[:].rearrange("p j t -> p (j t)")
-        )
+        for h in range(2):
+            cols = slice(h * HALF, (h + 1) * HALF)
+            nc.vector.quantize_mx(
+                out=x_codes[:, cols].bitcast(FP8X4),
+                scales=x_scales[:, cols],
+                in_=x_woven[h][:].rearrange("p j t -> p (j t)"),
+            )
 
         own = keep.tile([P, PACK, J], F32, align_bytes=64)
         read = keep.tile([P, PACK, J], F32, align_bytes=64)
-        sums = [psum.tile([P, J], F32, name="a%d" % t) for t in range(PACK)]
-        for t in range(PACK):
+        banks = {}
+
+        def hidden(t, lo, hi):
+            banks[t, lo] = psum.tile([P, hi - lo], F32, name="a%d_%d" % (t, lo))
             nc.tensor.matmul_mx(
-                out=sums[t][:],
+                out=banks[t, lo][:],
                 lhsT=wt_codes[:, t, :].bitcast(U8).bitcast(FP4X4),
                 lhsT_scale=wt_bytes[:, t, :],
-                rhs=x_codes[:].bitcast(FP8X4),
-                rhs_scale=x_scales[:],
+                rhs=x_codes[:, lo:hi].bitcast(FP8X4),
+                rhs_scale=x_scales[:, lo:hi],
                 start=True,
                 stop=True,
             )
+
+        for h in range(2):
+            for t in range(2):
+                hidden(t, h * HALF, (h + 1) * HALF)
+        for t in range(2, PACK):
+            hidden(t, 0, J)
+
+        def put_scalar(t, lo, hi):
+            nc.scalar.activation(
+                out=boards[t][:].indirect(list_put[:, lo // 16 : hi // 16]), in_=own[:, t, lo:hi], func=COPY
+            )
+
+        def put_vector(t, lo, hi):
+            nc.vector.tensor_copy(boards[t][:].indirect(list_put[:, lo // 16 : hi // 16]), own[:, t, lo:hi])
 
         def fetch(t, lo, hi):
             nc.scalar.activation(
@@ -127,17 +155,17 @@ def tile_list_boardownweighed_codedstore_one_plain_kernel(
                 scale=weights[:, t : t + 1],
             )
 
-        nc.vector.tensor_copy(out=own[:, 0, :], in_=sums[0][:])
-        nc.scalar.copy(out=own[:, 1, :], in_=sums[1][:])
-        nc.vector.tensor_copy(boards[0][:].indirect(list_put[:]), own[:, 0, :])
-        nc.scalar.activation(out=boards[1][:].indirect(list_put[:]), in_=own[:, 1, :], func=COPY)
-        nc.vector.tensor_copy(out=own[:, 2, :], in_=sums[2][:])
-        nc.scalar.copy(out=own[:, 3, :], in_=sums[3][:])
-        nc.vector.tensor_copy(boards[2][:].indirect(list_put[:]), own[:, 2, :])
-        nc.scalar.activation(
-            out=boards[3][:].indirect(list_put[:, 0 : SPLIT // 16]), in_=own[:, 3, 0:SPLIT], func=COPY
-        )
-        nc.vector.tensor_copy(boards[3][:].indirect(list_put[:, SPLIT // 16 : J // 16]), own[:, 3, SPLIT:J])
+        for h in range(2):
+            lo, hi = h * HALF, (h + 1) * HALF
+            nc.scalar.copy(out=own[:, 0, lo:hi], in_=banks[0, lo][:])
+            nc.vector.tensor_copy(out=own[:, 1, lo:hi], in_=banks[1, lo][:])
+            put_scalar(0, lo, hi)
+            put_vector(1, lo, min(hi, SPLIT))
+        nc.vector.tensor_copy(out=own[:, 2, :], in_=banks[2, 0][:])
+        nc.scalar.copy(out=own[:, 3, :], in_=banks[3, 0][:])
+        put_scalar(1, SPLIT, J)
+        put_vector(2, 0, J)
+        put_vector(3, 0, J)
         for t in range(PACK - 1):
             fetch(t, 0, J)
         for h in range(2):
@@ -162,7 +190,7 @@ def tile_list_boardownweighed_codedstore_one_plain_kernel(
             )
             result = keep.tile([P, N // P, HALF], F32, name="result%d" % h, align_bytes=64)
             for m in range(N // P):
-                y = psum.tile([P, HALF], F32, name="y%d%d" % (h, m))
+                y = psum.tile([P, HALF], F32, name="y%d%d" % (h, m), tag="a%d_%d" % (m, h * HALF))
                 nc.tensor.matmul_mx(
                     out=y[:],
                     lhsT=wb_codes[:, 2 * P * m : 2 * P * (m + 1)].bitcast(FP4X4),

@@ -19,18 +19,12 @@ MAX = mybir.AluOpType.max
 P = 128
 PACK = 4
 QUADS = 4
+QUAD_ROWS = 4
+PER_COLUMN = 16
+RUN = 4
 HALF = J // 2
-SPLIT = 192
+PUT_SPLIT = 96
 WEAVE_SPLIT = 192
-
-
-def spread_scale_rows(nc, plane, stage):
-    width = plane.shape[1] // 4
-    for q in range(QUADS):
-        nc.vector.tensor_copy(
-            out=plane[:].bitcast(I32)[32 * q : 32 * q + 4, :],
-            in_=stage[:, q * width : (q + 1) * width],
-        )
 
 
 def tile_list_boardownweighed_codedstore_one_plain_kernel(
@@ -41,42 +35,42 @@ def tile_list_boardownweighed_codedstore_one_plain_kernel(
         keep = ctx.enter_context(tc.tile_pool(name="keep", bufs=1))
         psum = ctx.enter_context(tc.psum_pool(name="psum", bufs=1))
 
-        list_x = keep.tile([P, J // 16], U16)
-        list_w = keep.tile([P, R // 16], U16)
-        list_put = keep.tile([P, J // 16], U16)
-        list_get = keep.tile([P, J // 16], U16)
-        wt_win = keep.tile([P, V], U16, align_bytes=64)
-        wt_stage = keep.tile([4, QUADS * V // 4], I32, align_bytes=64)
+        list_x = keep.tile([P, J // PER_COLUMN], U16)
+        list_w = keep.tile([P, R // PER_COLUMN], U16)
+        list_put = keep.tile([P, J // PER_COLUMN], U16)
+        list_get = keep.tile([P, J // PER_COLUMN], U16)
+        wt_table = keep.tile([P, V], U16, align_bytes=64)
+        wt_staged = keep.tile([QUAD_ROWS, QUADS * V // 4], I32, align_bytes=64)
         wb_codes = keep.tile([P, 2 * N], U8, align_bytes=64)
         steps = keep.tile([P, PACK], F32)
         weights = keep.tile([P, PACK], F32)
-        cq_rows = [keep.tile([P, T], F32, name="cq%d" % t, align_bytes=64) for t in range(PACK)]
-        cq_planes = cq.rearrange("(p t) c -> t p c", t=PACK)
+        cq_planes = [keep.tile([P, T], F32, name="cq%d" % t, align_bytes=64) for t in range(PACK)]
+        cq_rows = cq.rearrange("(p t) c -> t p c", t=PACK)
 
-        nc.sync.dma_start(out=cq_rows[0][:], in_=cq_planes[0])
+        nc.sync.dma_start(out=cq_planes[0][:], in_=cq_rows[0])
         nc.sync.dma_start(list_x[:], offs)
         nc.sync.dma_start(out=steps[:], in_=ga.rearrange("(p t) o -> p (t o)", t=PACK))
-        nc.sync.dma_start(out=wt_win[:].bitcast(I32), in_=wt_words[0].bitcast(I32))
+        nc.sync.dma_start(out=wt_table[:].bitcast(I32), in_=wt_words[0].bitcast(I32))
         nc.sync.dma_start(list_w[:], offs2)
         nc.sync.dma_start(
-            out=wt_stage[:].rearrange("r (q c) -> r q c", q=QUADS),
-            in_=wt_scales[0].bitcast(I32).rearrange("(q r) c -> r q c", q=QUADS),
+            out=wt_staged[:].rearrange("s (q c) -> s q c", q=QUADS),
+            in_=wt_scales[0].bitcast(I32).rearrange("(q s) c -> s q c", q=QUADS),
         )
         for t in range(1, PACK):
-            nc.sync.dma_start(out=cq_rows[t][:], in_=cq_planes[t])
+            nc.sync.dma_start(out=cq_planes[t][:], in_=cq_rows[t])
         nc.sync.dma_start(out=weights[:], in_=sa.rearrange("(p t) o -> p (t o)", t=PACK))
         nc.sync.dma_start(list_put[:], offs3)
         nc.sync.dma_start(list_get[:], offs4)
         nc.sync.dma_start(out=wb_codes[:].bitcast(I32), in_=wb_words[0].bitcast(I32))
 
-        wt_plane = keep.tile([P, V], U8, align_bytes=64)
-        wb_plane = keep.tile([P, N], U8, align_bytes=64)
-        nc.vector.memset(wt_plane[:].bitcast(I32), 0)
-        nc.vector.memset(wb_plane[:].bitcast(I32), 0)
+        wt_scale_table = keep.tile([P, V], U8, align_bytes=64)
+        wb_scale_rows = keep.tile([P, N], U8, align_bytes=64)
+        nc.vector.memset(wt_scale_table[:].bitcast(I32), 0)
+        nc.vector.memset(wb_scale_rows[:].bitcast(I32), 0)
         for q in range(QUADS):
             nc.sync.dma_start(
-                out=wb_plane[:].bitcast(I32)[32 * q : 32 * q + 4, :],
-                in_=wb_scales[0].bitcast(I32)[4 * q : 4 * q + 4, :],
+                out=wb_scale_rows[:].bitcast(I32)[32 * q : 32 * q + QUAD_ROWS, :],
+                in_=wb_scales[0].bitcast(I32)[QUAD_ROWS * q : QUAD_ROWS * (q + 1), :],
             )
         boards = [keep.tile([P, C], F32, name="board%d" % t, align_bytes=64) for t in range(PACK)]
         for t in range(PACK):
@@ -84,29 +78,36 @@ def tile_list_boardownweighed_codedstore_one_plain_kernel(
 
         wt_picked = keep.tile([P, R], U16, align_bytes=64)
         wt_codes = keep.tile([P, PACK, P], U16, align_bytes=64)
-        wt_bytes = keep.tile([P, PACK, P], U8, align_bytes=64)
-        nc.vector.tensor_copy(wt_picked[:], wt_win[:].indirect(list_w[:]))
-        nc.vector.tensor_copy(out=wt_codes[:], in_=wt_picked[:].rearrange("p (q t) -> p t q", t=PACK))
-        spread_scale_rows(nc, wt_plane, wt_stage)
-        nc.vector.tensor_copy(wt_bytes[:].rearrange("p t q -> p q t"), wt_plane[:].indirect(list_w[:]))
+        wt_scale_rows = keep.tile([P, PACK, P], U8, align_bytes=64)
+        nc.vector.tensor_copy(wt_picked[:], wt_table[:].indirect(list_w[:]))
+        nc.vector.tensor_copy(out=wt_codes[:], in_=wt_picked[:].rearrange("p (e t) -> p t e", t=PACK))
+        for q in range(QUADS):
+            nc.vector.tensor_copy(
+                out=wt_scale_table[:].bitcast(I32)[32 * q : 32 * q + QUAD_ROWS, :],
+                in_=wt_staged[:, q * V // 4 : (q + 1) * V // 4],
+            )
+        nc.vector.tensor_copy(wt_scale_rows[:].rearrange("p t e -> p e t"), wt_scale_table[:].indirect(list_w[:]))
 
         x_planes = keep.tile([P, PACK, J], BF16, align_bytes=64)
         for t in range(PACK):
             nc.scalar.activation(
-                out=x_planes[:, t, :], in_=cq_rows[t][:].indirect(list_x[:]), func=COPY, scale=steps[:, t : t + 1]
+                out=x_planes[:, t, :], in_=cq_planes[t][:].indirect(list_x[:]), func=COPY, scale=steps[:, t : t + 1]
             )
         x_woven = [keep.tile([P, HALF, PACK], BF16, name="x_woven%d" % h, align_bytes=64) for h in range(2)]
 
-        def weave(copy, lo, hi):
-            h, base = lo // HALF, lo // HALF * HALF
-            copy(
-                out=x_woven[h][:, lo - base : hi - base, :].rearrange("p (c i) t -> p c t i", i=4),
-                in_=x_planes[:, :, lo:hi].rearrange("p t (c i) -> p c t i", i=4),
-            )
+        def by_runs(planes, lo, hi):
+            return planes[:, :, lo:hi].rearrange("p t (c i) -> p c t i", i=RUN)
 
-        weave(nc.vector.tensor_copy, 0, HALF)
-        weave(nc.vector.tensor_copy, HALF, WEAVE_SPLIT)
-        weave(nc.scalar.copy, WEAVE_SPLIT, J)
+        def woven_by_runs(woven, lo, hi):
+            h = lo // HALF
+            return woven[h][:, lo - h * HALF : hi - h * HALF, :].rearrange("p (c i) t -> p c t i", i=RUN)
+
+        for copy, lo, hi in (
+            (nc.vector.tensor_copy, 0, HALF),
+            (nc.vector.tensor_copy, HALF, WEAVE_SPLIT),
+            (nc.scalar.copy, WEAVE_SPLIT, J),
+        ):
+            copy(out=woven_by_runs(x_woven, lo, hi), in_=by_runs(x_planes, lo, hi))
         x_codes = keep.tile([P, J], U32, align_bytes=64)
         x_scales = keep.tile([P, J], U8, align_bytes=64)
         for h in range(2):
@@ -126,7 +127,7 @@ def tile_list_boardownweighed_codedstore_one_plain_kernel(
             nc.tensor.matmul_mx(
                 out=banks[t, lo][:],
                 lhsT=wt_codes[:, t, :].bitcast(U8).bitcast(FP4X4),
-                lhsT_scale=wt_bytes[:, t, :],
+                lhsT_scale=wt_scale_rows[:, t, :],
                 rhs=x_codes[:, lo:hi].bitcast(FP8X4),
                 rhs_scale=x_scales[:, lo:hi],
                 start=True,
@@ -139,18 +140,21 @@ def tile_list_boardownweighed_codedstore_one_plain_kernel(
         for t in range(2, PACK):
             hidden(t, 0, J)
 
+        def entries(list_tile, lo, hi):
+            return list_tile[:, lo // PER_COLUMN : hi // PER_COLUMN]
+
         def put_scalar(t, lo, hi):
             nc.scalar.activation(
-                out=boards[t][:].indirect(list_put[:, lo // 16 : hi // 16]), in_=own[:, t, lo:hi], func=COPY
+                out=boards[t][:].indirect(entries(list_put, lo, hi)), in_=own[:, t, lo:hi], func=COPY
             )
 
         def put_vector(t, lo, hi):
-            nc.vector.tensor_copy(boards[t][:].indirect(list_put[:, lo // 16 : hi // 16]), own[:, t, lo:hi])
+            nc.vector.tensor_copy(boards[t][:].indirect(entries(list_put, lo, hi)), own[:, t, lo:hi])
 
         def fetch(t, lo, hi):
             nc.scalar.activation(
                 out=read[:, t, lo:hi],
-                in_=boards[t][:].indirect(list_get[:, lo // 16 : hi // 16]),
+                in_=boards[t][:].indirect(entries(list_get, lo, hi)),
                 func=COPY,
                 scale=weights[:, t : t + 1],
             )
@@ -160,10 +164,11 @@ def tile_list_boardownweighed_codedstore_one_plain_kernel(
             nc.scalar.copy(out=own[:, 0, lo:hi], in_=banks[0, lo][:])
             nc.vector.tensor_copy(out=own[:, 1, lo:hi], in_=banks[1, lo][:])
             put_scalar(0, lo, hi)
-            put_vector(1, lo, min(hi, SPLIT))
+            if lo < PUT_SPLIT:
+                put_vector(1, lo, PUT_SPLIT)
         nc.vector.tensor_copy(out=own[:, 2, :], in_=banks[2, 0][:])
         nc.scalar.copy(out=own[:, 3, :], in_=banks[3, 0][:])
-        put_scalar(1, SPLIT, J)
+        put_scalar(1, PUT_SPLIT, J)
         put_vector(2, 0, J)
         put_vector(3, 0, J)
         for t in range(PACK - 1):
@@ -171,22 +176,20 @@ def tile_list_boardownweighed_codedstore_one_plain_kernel(
         for h in range(2):
             fetch(PACK - 1, h * HALF, (h + 1) * HALF)
 
-        out_rows = out.rearrange("(m p) j -> p m j", p=P)
-        woven = [keep.tile([P, HALF, PACK], BF16, name="hid%d" % h, align_bytes=64) for h in range(2)]
+        h_woven = [keep.tile([P, HALF, PACK], BF16, name="h_woven%d" % h, align_bytes=64) for h in range(2)]
         for h in range(2):
-            cols = slice(h * HALF, (h + 1) * HALF)
+            lo, hi = h * HALF, (h + 1) * HALF
             nc.vector.tensor_tensor(
-                out=woven[h][:].rearrange("p (c i) t -> p c t i", i=4),
-                in0=read[:, :, cols].rearrange("p t (c i) -> p c t i", i=4),
-                in1=own[:, :, cols].rearrange("p t (c i) -> p c t i", i=4),
-                op=MAX,
+                out=woven_by_runs(h_woven, lo, hi), in0=by_runs(read, lo, hi), in1=by_runs(own, lo, hi), op=MAX
             )
+
+        out_rows = out.rearrange("(m p) j -> p m j", p=P)
         for h in range(2):
             cols = slice(h * HALF, (h + 1) * HALF)
             h_codes = keep.tile([P, HALF], U32, name="h_codes%d" % h, align_bytes=64)
             h_scales = keep.tile([P, HALF], U8, name="h_scales%d" % h, align_bytes=64)
             nc.vector.quantize_mx(
-                out=h_codes[:].bitcast(FP8X4), scales=h_scales[:], in_=woven[h][:].rearrange("p j t -> p (j t)")
+                out=h_codes[:].bitcast(FP8X4), scales=h_scales[:], in_=h_woven[h][:].rearrange("p j t -> p (j t)")
             )
             result = keep.tile([P, N // P, HALF], F32, name="result%d" % h, align_bytes=64)
             for m in range(N // P):
@@ -194,14 +197,12 @@ def tile_list_boardownweighed_codedstore_one_plain_kernel(
                 nc.tensor.matmul_mx(
                     out=y[:],
                     lhsT=wb_codes[:, 2 * P * m : 2 * P * (m + 1)].bitcast(FP4X4),
-                    lhsT_scale=wb_plane[:, P * m : P * (m + 1)],
+                    lhsT_scale=wb_scale_rows[:, P * m : P * (m + 1)],
                     rhs=h_codes[:].bitcast(FP8X4),
                     rhs_scale=h_scales[:],
                     start=True,
                     stop=True,
                 )
-                if h == 1 and m == 1:
-                    nc.vector.tensor_copy(out=result[:, m, :], in_=y[:])
-                else:
-                    nc.scalar.copy(out=result[:, m, :], in_=y[:])
+                last_bank = h == 1 and m == N // P - 1
+                (nc.vector.tensor_copy if last_bank else nc.scalar.copy)(out=result[:, m, :], in_=y[:])
             nc.sync.dma_start(out=out_rows[:, :, cols], in_=result[:])

from contextlib import ExitStack

import concourse.mybir as mybir

K, T, J, R, V, C, N = 512, 1024, 256, 512, 1024, 512, 256
FLOPS = 2 * K * R * J + 2 * R * N * J

F32 = mybir.dt.float32
BF16 = mybir.dt.bfloat16
I32 = mybir.dt.int32
U32 = mybir.dt.uint32
U16 = mybir.dt.uint16
U8 = mybir.dt.uint8
FP8X4 = mybir.dt.float8_e4m3fn_x4
FP4X4 = mybir.dt.float4_e2m1fn_x4
COPY = mybir.ActivationFunctionType.Copy
MAX = mybir.AluOpType.max

P = 128
PACK = 4
QUADS = 4
QUAD_ROWS = 4
PER_COLUMN = 16
RUN = 4
HALF = J // 2
PUT_SPLIT = 96
WEAVE_SPLIT = 192


def tile_list_boardownweighed_codedstore_one_plain_kernel(
    tc, cq, ga, wt_words, wt_scales, sa, wb_words, wb_scales, offs, offs2, offs3, offs4, out
):
    nc = tc.nc
    with ExitStack() as ctx:
        keep = ctx.enter_context(tc.tile_pool(name="keep", bufs=1))
        psum = ctx.enter_context(tc.psum_pool(name="psum", bufs=1))

        list_x = keep.tile([P, J // PER_COLUMN], U16)
        list_w = keep.tile([P, R // PER_COLUMN], U16)
        list_put = keep.tile([P, J // PER_COLUMN], U16)
        list_get = keep.tile([P, J // PER_COLUMN], U16)
        wt_table = keep.tile([P, V], U16, align_bytes=64)
        wt_staged = keep.tile([QUAD_ROWS, QUADS * V // 4], I32, align_bytes=64)
        wb_codes = keep.tile([P, 2 * N], U8, align_bytes=64)
        steps = keep.tile([P, PACK], F32)
        weights = keep.tile([P, PACK], F32)
        cq_planes = [keep.tile([P, T], F32, name="cq%d" % t, align_bytes=64) for t in range(PACK)]
        cq_rows = cq.rearrange("(p t) c -> t p c", t=PACK)

        nc.sync.dma_start(out=cq_planes[0][:], in_=cq_rows[0])
        nc.sync.dma_start(list_x[:], offs)
        nc.sync.dma_start(out=steps[:], in_=ga.rearrange("(p t) o -> p (t o)", t=PACK))
        nc.sync.dma_start(out=wt_table[:].bitcast(I32), in_=wt_words[0].bitcast(I32))
        nc.sync.dma_start(list_w[:], offs2)
        nc.sync.dma_start(
            out=wt_staged[:].rearrange("s (q c) -> s q c", q=QUADS),
            in_=wt_scales[0].bitcast(I32).rearrange("(q s) c -> s q c", q=QUADS),
        )
        for t in range(1, PACK):
            nc.sync.dma_start(out=cq_planes[t][:], in_=cq_rows[t])
        nc.sync.dma_start(out=weights[:], in_=sa.rearrange("(p t) o -> p (t o)", t=PACK))
        nc.sync.dma_start(list_put[:], offs3)
        nc.sync.dma_start(list_get[:], offs4)
        nc.sync.dma_start(out=wb_codes[:].bitcast(I32), in_=wb_words[0].bitcast(I32))

        wt_scale_table = keep.tile([P, V], U8, align_bytes=64)
        wb_scale_rows = keep.tile([P, N], U8, align_bytes=64)
        nc.vector.memset(wt_scale_table[:].bitcast(I32), 0)
        nc.vector.memset(wb_scale_rows[:].bitcast(I32), 0)
        for q in range(QUADS):
            nc.sync.dma_start(
                out=wb_scale_rows[:].bitcast(I32)[32 * q : 32 * q + QUAD_ROWS, :],
                in_=wb_scales[0].bitcast(I32)[QUAD_ROWS * q : QUAD_ROWS * (q + 1), :],
            )
        boards = [keep.tile([P, C], F32, name="board%d" % t, align_bytes=64) for t in range(PACK)]
        for t in range(PACK):
            nc.vector.memset(boards[t][:], 0.0)

        wt_picked = keep.tile([P, R], U16, align_bytes=64)
        wt_codes = keep.tile([P, PACK, P], U16, align_bytes=64)
        wt_scale_rows = keep.tile([P, PACK, P], U8, align_bytes=64)
        nc.vector.tensor_copy(wt_picked[:], wt_table[:].indirect(list_w[:]))
        nc.vector.tensor_copy(out=wt_codes[:], in_=wt_picked[:].rearrange("p (e t) -> p t e", t=PACK))
        for q in range(QUADS):
            nc.vector.tensor_copy(
                out=wt_scale_table[:].bitcast(I32)[32 * q : 32 * q + QUAD_ROWS, :],
                in_=wt_staged[:, q * V // 4 : (q + 1) * V // 4],
            )
        nc.vector.tensor_copy(wt_scale_rows[:].rearrange("p t e -> p e t"), wt_scale_table[:].indirect(list_w[:]))

        x_planes = keep.tile([P, PACK, J], BF16, align_bytes=64)
        for t in range(PACK):
            nc.scalar.activation(
                out=x_planes[:, t, :], in_=cq_planes[t][:].indirect(list_x[:]), func=COPY, scale=steps[:, t : t + 1]
            )
        x_woven = [keep.tile([P, HALF, PACK], BF16, name="x_woven%d" % h, align_bytes=64) for h in range(2)]

        def by_runs(planes, lo, hi):
            return planes[:, :, lo:hi].rearrange("p t (c i) -> p c t i", i=RUN)

        def woven_by_runs(woven, lo, hi):
            h = lo // HALF
            return woven[h][:, lo - h * HALF : hi - h * HALF, :].rearrange("p (c i) t -> p c t i", i=RUN)

        for copy, lo, hi in (
            (nc.vector.tensor_copy, 0, HALF),
            (nc.vector.tensor_copy, HALF, WEAVE_SPLIT),
            (nc.scalar.copy, WEAVE_SPLIT, J),
        ):
            copy(out=woven_by_runs(x_woven, lo, hi), in_=by_runs(x_planes, lo, hi))
        x_codes = keep.tile([P, J], U32, align_bytes=64)
        x_scales = keep.tile([P, J], U8, align_bytes=64)
        for h in range(2):
            cols = slice(h * HALF, (h + 1) * HALF)
            nc.vector.quantize_mx(
                out=x_codes[:, cols].bitcast(FP8X4),
                scales=x_scales[:, cols],
                in_=x_woven[h][:].rearrange("p j t -> p (j t)"),
            )

        own = keep.tile([P, PACK, J], F32, align_bytes=64)
        read = keep.tile([P, PACK, J], F32, align_bytes=64)
        banks = {}

        def hidden(t, lo, hi):
            banks[t, lo] = psum.tile([P, hi - lo], F32, name="a%d_%d" % (t, lo))
            nc.tensor.matmul_mx(
                out=banks[t, lo][:],
                lhsT=wt_codes[:, t, :].bitcast(U8).bitcast(FP4X4),
                lhsT_scale=wt_scale_rows[:, t, :],
                rhs=x_codes[:, lo:hi].bitcast(FP8X4),
                rhs_scale=x_scales[:, lo:hi],
                start=True,
                stop=True,
            )

        for h in range(2):
            for t in range(2):
                hidden(t, h * HALF, (h + 1) * HALF)
        for t in range(2, PACK):
            hidden(t, 0, J)

        def entries(list_tile, lo, hi):
            return list_tile[:, lo // PER_COLUMN : hi // PER_COLUMN]

        def put_scalar(t, lo, hi):
            nc.scalar.activation(
                out=boards[t][:].indirect(entries(list_put, lo, hi)), in_=own[:, t, lo:hi], func=COPY
            )

        def put_vector(t, lo, hi):
            nc.vector.tensor_copy(boards[t][:].indirect(entries(list_put, lo, hi)), own[:, t, lo:hi])

        def fetch(t, lo, hi):
            nc.scalar.activation(
                out=read[:, t, lo:hi],
                in_=boards[t][:].indirect(entries(list_get, lo, hi)),
                func=COPY,
                scale=weights[:, t : t + 1],
            )

        for h in range(2):
            lo, hi = h * HALF, (h + 1) * HALF
            nc.scalar.copy(out=own[:, 0, lo:hi], in_=banks[0, lo][:])
            nc.vector.tensor_copy(out=own[:, 1, lo:hi], in_=banks[1, lo][:])
            put_scalar(0, lo, hi)
            if lo < PUT_SPLIT:
                put_vector(1, lo, PUT_SPLIT)
        nc.vector.tensor_copy(out=own[:, 2, :], in_=banks[2, 0][:])
        nc.scalar.copy(out=own[:, 3, :], in_=banks[3, 0][:])
        put_scalar(1, PUT_SPLIT, J)
        put_vector(2, 0, J)
        put_vector(3, 0, J)
        for t in range(PACK - 1):
            fetch(t, 0, J)
        for h in range(2):
            fetch(PACK - 1, h * HALF, (h + 1) * HALF)

        h_woven = [keep.tile([P, HALF, PACK], BF16, name="h_woven%d" % h, align_bytes=64) for h in range(2)]
        for h in range(2):
            lo, hi = h * HALF, (h + 1) * HALF
            nc.vector.tensor_tensor(
                out=woven_by_runs(h_woven, lo, hi), in0=by_runs(read, lo, hi), in1=by_runs(own, lo, hi), op=MAX
            )

        out_rows = out.rearrange("(m p) j -> p m j", p=P)
        for h in range(2):
            cols = slice(h * HALF, (h + 1) * HALF)
            h_codes = keep.tile([P, HALF], U32, name="h_codes%d" % h, align_bytes=64)
            h_scales = keep.tile([P, HALF], U8, name="h_scales%d" % h, align_bytes=64)
            nc.vector.quantize_mx(
                out=h_codes[:].bitcast(FP8X4), scales=h_scales[:], in_=h_woven[h][:].rearrange("p j t -> p (j t)")
            )
            result = keep.tile([P, N // P, HALF], F32, name="result%d" % h, align_bytes=64)
            for m in range(N // P):
                y = psum.tile([P, HALF], F32, name="y%d%d" % (h, m), tag="a%d_%d" % (m, h * HALF))
                nc.tensor.matmul_mx(
                    out=y[:],
                    lhsT=wb_codes[:, 2 * P * m : 2 * P * (m + 1)].bitcast(FP4X4),
                    lhsT_scale=wb_scale_rows[:, P * m : P * (m + 1)],
                    rhs=h_codes[:].bitcast(FP8X4),
                    rhs_scale=h_scales[:],
                    start=True,
                    stop=True,
                )
                last_bank = h == 1 and m == N // P - 1
                (nc.vector.tensor_copy if last_bank else nc.scalar.copy)(out=result[:, m, :], in_=y[:])
            nc.sync.dma_start(out=out_rows[:, :, cols], in_=result[:])
